import numpy as np, ml_dtypes
CORES = [16,17,18,19,150,151]
N = 6
import mx_ref
NC, G = 384, 4
C = np.float32(0.029)
WID = [384,128,192,288,128,160]
BF = ml_dtypes.bfloat16
def cut(t, i, w=512):
    return t[:, w * i:w * i + w]
def tile(rs):
    return np.stack(rs, axis=2).reshape(128, -1).astype(BF)
def layer(w, X):
    out = []
    for i in range(G):
        for t in range(len(X)):
            p = mx_ref.matmul(mx_ref.quantize(cut(w, len(X) * i + t)), X[t])
            z = p if t == 0 else z + p
        out.append(z)
    return out
def act(Z):
    return [np.maximum(z, 0) * C for z in Z]
def setup_inputs(rng):
    def f(*shape):
        return mx_ref.flush((rng.standard_normal(shape, dtype=np.float32) * np.exp2(rng.integers(-2, 3, shape[:-1] + (1,)))).astype(BF))
    return {"x": f(N, 128, 4 * NC), "w1": f(N, 128, G * 512), "w2": f(N, 128, 512)}
def setup_inputs_blocks(rng):
    d = setup_inputs(rng)
    for k in ("x", "w1", "w2"): d[k] = mx_ref.spread(d[k], rng, 2)
    return d
def setup_inputs_wide(rng):
    d = setup_inputs(rng)
    for k in ("x", "w1", "w2"): d[k] = mx_ref.flush((d[k].astype(np.float32) * np.exp2(rng.integers(-6, 7, (N, 1, 1))).astype(np.float32)).astype(BF))
    return d
def reference(x, w1, w2):
    X = [mx_ref.quantize(x[j][:, :4 * WID[j]]) for j in range(N)]
    y = np.full((N, 128, NC), np.nan, np.float32)
    for c in range(N):
        for r in range(N):
            p = mx_ref.matmul(mx_ref.quantize(w2[r]), mx_ref.quantize(tile(act(layer(w1[r], [X[c]])))))
            z = p if r == 0 else z + p
        y[c][:, :WID[c]] = z
    return {"y": y}

@@ -1,0 +1,296 @@
+from concourse.bass import DstId, RemoteDMATransfer
+from concourse.mybir import dt, AluOpType, ActivationFunctionType
+
+U8 = dt.uint8
+SCRATCH = {
+    "xraw": ("sbuf", [128, 1536], "bfloat16"),
+    "wraw": ("sbuf", [128, 2560], "bfloat16"),
+    "xq": ("sbuf", [128, 640], "float8_e4m3fn_x4"),
+    "xs": ("sbuf", [128, 640], "uint8"),
+    "wq0": ("sbuf", [128, 640], "float8_e4m3fn_x4"),
+    "ws0": ("sbuf", [128, 640], "uint8"),
+    "wq1": ("sbuf", [128, 640], "float8_e4m3fn_x4"),
+    "ws1": ("sbuf", [128, 640], "uint8"),
+    "h0": ("sbuf", [128, 2560], "bfloat16"),
+    "h1": ("sbuf", [128, 2560], "bfloat16"),
+    "hq0": ("sbuf", [128, 640], "float8_e4m3fn_x4"),
+    "hs0": ("sbuf", [128, 640], "uint8"),
+    "hq1": ("sbuf", [128, 640], "float8_e4m3fn_x4"),
+    "hs1": ("sbuf", [128, 640], "uint8"),
+    "yout": ("sbuf", [128, 640], "float32"),
+    "yin0": ("sbuf", [128, 384], "float32"),
+    "yin1": ("sbuf", [128, 384], "float32"),
+    "acc": ("sbuf", [128, 384], "float32"),
+    "fin": ("sbuf", [128, 384], "float32"),
+    "ps": ("psum", [128, 4096], "float32"),
+}
+ZB = 6
+LATE = 2
+C = 0.029
+SEMAPHORES = (["ld%d" % i for i in range(5)] + ["st%d" % i for i in range(2)]
+              + ["ar_x0", "ar_x1", "ar_x2", "ar_w", "ls", "te", "ve", "sc"]
+              + ["ar_y%d_%d" % (s, b) for s in range(2) for b in range(2)])
+
+
+def grid(T, topo):
+    wid, cores, n = T.tables["WID"], T.cores, len(T.cores)
+    half = sum(wid) // 2
+
+    def home(r):
+        return (topo.host(cores[r]), topo.chip(cores[r]))
+    for bits in range(1, 1 << n, 2):
+        a = [r for r in range(n) if bits >> r & 1]
+        b = [r for r in range(n) if not bits >> r & 1]
+        if len(a) != len(b) or sum(wid[r] for r in a) != half:
+            continue
+        left, pairs = list(b), []
+        for r in a:
+            for q in left:
+                if home(q) == home(r):
+                    pairs.append(q)
+                    left.remove(q)
+                    break
+        if len(pairs) == len(a):
+            return a, pairs
+    raise ValueError("no grid")
+
+
+def count(m):
+    return bin(m).count("1")
+
+
+def rank_program(g, core, T, topo):
+    me = T.rank_of(core)
+    if me is None:
+        return
+    wid = T.tables["WID"]
+    ga, gb = grid(T, topo)
+    grp = ga if me in ga else gb
+    pos = grp.index(me)
+    peer = (gb if me in ga else ga)[pos]
+    others = [r for r in grp if r != me]
+    off = {}
+    o = 0
+    for r in grp:
+        off[r] = o
+        o += wid[r]
+
+    def blocks(r):
+        if wid[r] > 320:
+            return [(0, wid[r] // 2), (wid[r] // 2, wid[r] // 2)]
+        return [(0, wid[r])]
+
+    def cm(r):
+        return T.cores[r]
+
+    def xmasks(src):
+        ds = [r for r in grp if r != src]
+        ms = [topo.mask(cm(src), cm(d)) for d in ds]
+        if ms[0] != ms[1]:
+            i = 0 if count(ms[0]) > count(ms[1]) else 1
+            ms[i] &= ~ms[1 - i]
+        return ds, ms
+
+    def did(r):
+        rid, pid = topo.addr(cm(r), core)
+        return DstId(rid=rid, pnc=pid)
+
+    known, done = {}, {"te": 0, "ve": 0, "sc": 0}
+    final = []
+
+    def wait(qn, q, deps):
+        for tok in deps:
+            if tok is None:
+                continue
+            s, v = tok
+            if known.get((qn, s), 0) < v:
+                q.wait_ge(T.sem[s], v)
+                known[(qn, s)] = v
+
+    def run(qn, q, deps, fn):
+        wait(qn, q, deps)
+        fn().then_inc(T.sem[qn], 1)
+        done[qn] += 1
+        return (qn, done[qn])
+
+    def te(deps, fn):
+        return run("te", g.tensor, deps, fn)
+
+    def ve(deps, fn):
+        return run("ve", g.vector, deps, fn)
+
+    def sc(deps, fn):
+        return run("sc", g.scalar, deps, fn)
+
+    dmaq = [("sync", g.sync), ("sc", g.scalar)]
+
+    nb = blocks(me)
+    loads = [("x", a, n) for a, n in nb] + [("w", 0, 256), ("w", 256, 256), ("w2", 512, 128)]
+    ltok = []
+    for i, (k, a, n) in enumerate(loads):
+        s = "ld%d" % i
+        q = dmaq[i % 2][1]
+        if k == "x":
+            q.dma_start(T.xraw[:, 4 * a:4 * (a + n)], T.x[:, 4 * a:4 * (a + n)]).then_inc(T.sem[s], 16)
+        elif k == "w":
+            q.dma_start(T.wraw[:, 4 * a:4 * (a + n)], T.w1[:, 4 * a:4 * (a + n)]).then_inc(T.sem[s], 16)
+        else:
+            q.dma_start(T.wraw[:, 4 * a:4 * (a + n)], T.w2[:, 0:4 * n]).then_inc(T.sem[s], 16)
+        ltok.append((s, 16))
+    xtok, wtok = None, []
+    for i, (k, a, n) in enumerate(loads):
+        if k == "x":
+            oo = off[me] + a
+            xtok = ve([ltok[i]], lambda: g.vector.quantize_mx(
+                T.xq[:, oo:oo + n], T.xs[:, oo:oo + n], T.xraw[:, 4 * a:4 * (a + n)]))
+        else:
+            wtok.append(ve([ltok[i]], lambda: g.vector.quantize_mx(
+                T.wq0[:, a:a + n], T.ws0[:, a:a + n], T.wraw[:, 4 * a:4 * (a + n)])))
+
+    nls = [0]
+    o0, o1 = off[me], off[me] + wid[me]
+
+    def fused(trs):
+        g.remote_dma_fused(trs, local_sem=T.sem["ls"])
+
+    wait("g", g, [xtok])
+    ds, ms = xmasks(me)
+    rs = T.sem["ar_x%d" % pos]
+    for codes in (True, False):
+        def view():
+            return T.xq[:, o0:o1].bitcast(U8) if codes else T.xs[:, o0:o1]
+        if ms[0] == ms[1]:
+            fused([RemoteDMATransfer(dst_ids=[did(d) for d in ds], dma_engine_mask=ms[0], remote_sem=rs,
+                                     srcs=[view()], dsts=[view() for d in ds])])
+            nls[0] += count(ms[0])
+        else:
+            fused([RemoteDMATransfer(dst_ids=[did(d)], dma_engine_mask=m, remote_sem=rs,
+                                     srcs=[view()], dsts=[view()]) for d, m in zip(ds, ms)])
+            nls[0] += count(ms[0]) + count(ms[1])
+    wait("g", g, [wtok[-1]])
+    pm = topo.mask(core, cm(peer))
+    rid, pid = topo.addr(cm(peer), core)
+    g.remote_dma(T.wq1[:].bitcast(U8), T.wq0[:].bitcast(U8), T.sem["ar_w"], T.sem["ls"], pid, rid, pm)
+    g.remote_dma(T.ws1[:], T.ws0[:], T.sem["ar_w"], T.sem["ls"], pid, rid, pm)
+    nls[0] += 2 * count(pm)
+
+    xarr = {me: xtok}
+    for r in others:
+        d2, m2 = xmasks(r)
+        xarr[r] = ("ar_x%d" % grp.index(r), 2 * count(m2[d2.index(me)]))
+    warr = ("ar_w", 2 * count(topo.mask(cm(peer), core)))
+
+    own = (off[me], wid[me], [(me, 0, wid[me])])
+    big = sorted(others, key=lambda r: -wid[r])
+    oth = []
+    if sum(wid[r] for r in others) <= 256 and abs(grp.index(others[0]) - grp.index(others[1])) == 1:
+        oth.append([(off[others[0]], sum(wid[r] for r in others), [(r, 0, wid[r]) for r in others])])
+    else:
+        for r in big:
+            oth.append([(off[r] + a, n, [(r, a, n)]) for a, n in blocks(r)])
+    plan = [(0, own)]
+    for chunks in oth:
+        plan += [(0, ch) for ch in chunks]
+        plan += [(1, ch) for ch in chunks]
+    plan.append((1, own))
+
+    zfree = [None] * ZB
+    yfree = [None] * 2
+    zi, yi, ui = [0], [0], [0]
+    hq = {}
+
+    def bank(b, n):
+        return T.ps[:, 512 * b:512 * b + n]
+
+    def unit(side, ch, between):
+        a, n, parts = ch
+        W, S, H, HQ, HS = [(T.wq0, T.ws0, T.h0, T.hq0, T.hs0), (T.wq1, T.ws1, T.h1, T.hq1, T.hs1)][side]
+        xdeps = [xarr[r] for r, p, m in parts]
+        acts = []
+        ui[0] += 1
+        for b in range(4):
+            if b == LATE:
+                between()
+            k = zi[0] % ZB
+            zi[0] += 1
+            wd = warr if side else wtok[b // 2]
+            z = te([wd, zfree[k]] + xdeps, lambda: g.tensor.matmul_mx(
+                bank(k, n), W[:, 128 * b:128 * b + 128], S[:, 128 * b:128 * b + 128],
+                T.xq[:, a:a + n], T.xs[:, a:a + n], True, True))
+            onv = b in ((1, 3) if ui[0] % 2 else (2,))
+            if onv:
+                t = ve([z], lambda: g.vector.tensor_scalar(
+                    H[:, 4 * a + b:4 * (a + n):4], bank(k, n), 0.0, C, AluOpType.max, AluOpType.mult))
+            else:
+                t = sc([z], lambda: g.scalar.activation(
+                    H[:, 4 * a + b:4 * (a + n):4], bank(k, n), ActivationFunctionType.Relu, scale=C))
+            zfree[k] = t
+            acts.append(t)
+        hq[(side, a)] = ve(acts, lambda: g.vector.quantize_mx(
+            HQ[:, a:a + n], HS[:, a:a + n], H[:, 4 * a:4 * (a + n)]))
+
+    def second(ch):
+        a, n, parts = ch
+        k = yi[0] % 2
+        yi[0] += 1
+        te([wtok[-1], hq[(0, a)], yfree[k]], lambda: g.tensor.matmul_mx(
+            bank(ZB + k, n), T.wq0[:, 512:640], T.ws0[:, 512:640], T.hq0[:, a:a + n], T.hs0[:, a:a + n], True, False))
+        t = te([warr, hq[(1, a)]], lambda: g.tensor.matmul_mx(
+            bank(ZB + k, n), T.wq1[:, 512:640], T.ws1[:, 512:640], T.hq1[:, a:a + n], T.hs1[:, a:a + n], False, True))
+        return k, t
+
+    def ymask(src, dst):
+        return topo.mask(cm(src), cm(dst))
+
+    def finish(ch):
+        a, n, parts = ch
+        k, t = second(ch)
+        if parts[0][0] == me:
+            return k, t
+        cp = sc([t], lambda: g.scalar.activation(T.yout[:, a:a + n], bank(ZB + k, n), ActivationFunctionType.Copy))
+        yfree[k] = cp
+        wait("g", g, [cp])
+        for r, p, m in parts:
+            c0 = off[r] + p
+            slot = [q for q in grp if q != r].index(me)
+            bi = [x[0] for x in blocks(r)].index(p)
+            rid, pid = topo.addr(cm(r), core)
+            mk = ymask(me, r)
+            dst = T["yin%d" % slot]
+            g.remote_dma(dst[:, p:p + m], T.yout[:, c0:c0 + m], T.sem["ar_y%d_%d" % (slot, bi)], T.sem["ls"],
+                         pid, rid, mk)
+            nls[0] += count(mk)
+        return None
+
+    pend = [None]
+
+    def flush():
+        if pend[0] is not None:
+            finish(pend[0])
+            pend[0] = None
+
+    for side, ch in plan:
+        unit(side, ch, flush)
+        flush()
+        if side == 1:
+            pend[0] = ch
+    k, t = finish(pend[0])
+
+    near = sorted(range(2), key=lambda s: -count(topo.mask(cm(others[s]), core)))
+    fins = []
+    for bi, (a, n) in enumerate(nb):
+        s = near[0]
+        u = ve([t, ("ar_y%d_%d" % (s, bi), count(ymask(others[s], me)))], lambda: g.vector.tensor_tensor(
+            T.acc[:, a:a + n], T.ps[:, 512 * (ZB + k) + a:512 * (ZB + k) + a + n], T["yin%d" % s][:, a:a + n],
+            AluOpType.add))
+        fins.append(u)
+    for bi, (a, n) in enumerate(nb):
+        s = near[1]
+        u = ve([fins[bi], ("ar_y%d_%d" % (s, bi), count(ymask(others[s], me)))], lambda: g.vector.tensor_tensor(
+            T.fin[:, a:a + n], T.acc[:, a:a + n], T["yin%d" % s][:, a:a + n], AluOpType.add))
+        qn, q = dmaq[bi % 2]
+        wait(qn, q, [u])
+        q.dma_start(T.y[:, a:a + n], T.fin[:, a:a + n]).then_inc(T.sem["st%d" % bi], 16)
+        final.append(("st%d" % bi, 16))
+    final += [("ls", nls[0]), ("te", done["te"]), ("ve", done["ve"]), ("sc", done["sc"])]
+    wait("g", g, final)

@@ -24,11 +24,12 @@ SCRATCH = {
     "fin": ("sbuf", [128, 384], "float32"),
     "ps": ("psum", [128, 4096], "float32"),
 }
-ZB = 6
-LATE = 2
+CFG = dict(ZB=6, LATE=3, CUT=270, XCUT=270, far="oO sB oP", near="oO nO fO nP fP oP", near0="oO mB oP",
+           sfar="xc w xs", snear="xcs w", lfar="x w", lnear="x w", ON=((1, 3),), cp="sc")
 C = 0.029
 SEMAPHORES = (["ld%d" % i for i in range(5)] + ["st%d" % i for i in range(2)]
-              + ["ar_x0", "ar_x1", "ar_x2", "ar_w", "ls", "te", "ve", "sc"]
+              + ["ar_x%d_%d" % (s, b) for s in range(3) for b in range(2)]
+              + ["ar_w", "ls", "te", "ve", "sc"]
               + ["ar_y%d_%d" % (s, b) for s in range(2) for b in range(2)])
 
 
@@ -59,10 +60,15 @@ def count(m):
     return bin(m).count("1")
 
 
+def cut(n, limit):
+    return [(0, n // 2), (n // 2, n // 2)] if n > limit else [(0, n)]
+
+
 def rank_program(g, core, T, topo):
     me = T.rank_of(core)
     if me is None:
         return
+    ZB, LATE = CFG["ZB"], CFG["LATE"]
     wid = T.tables["WID"]
     ga, gb = grid(T, topo)
     grp = ga if me in ga else gb
@@ -76,16 +82,20 @@ def rank_program(g, core, T, topo):
         o += wid[r]
 
     def blocks(r):
-        if wid[r] > 320:
-            return [(0, wid[r] // 2), (wid[r] // 2, wid[r] // 2)]
-        return [(0, wid[r])]
+        return cut(wid[r], CFG["CUT"])
+
+    def xblocks(r):
+        return cut(wid[r], CFG["XCUT"])
 
     def cm(r):
         return T.cores[r]
 
+    def mask(a, b):
+        return topo.mask(cm(a), cm(b))
+
     def xmasks(src):
         ds = [r for r in grp if r != src]
-        ms = [topo.mask(cm(src), cm(d)) for d in ds]
+        ms = [mask(src, d) for d in ds]
         if ms[0] != ms[1]:
             i = 0 if count(ms[0]) > count(ms[1]) else 1
             ms[i] &= ~ms[1 - i]
@@ -94,6 +104,9 @@ def rank_program(g, core, T, topo):
     def did(r):
         rid, pid = topo.addr(cm(r), core)
         return DstId(rid=rid, pnc=pid)
+
+    on_chip = [r for r in others if mask(r, me) == mask(peer, me)]
+    role = "near" if on_chip else "far"
 
     known, done = {}, {"te": 0, "ve": 0, "sc": 0}
     final = []
@@ -125,38 +138,46 @@ def rank_program(g, core, T, topo):
     dmaq = [("sync", g.sync), ("sc", g.scalar)]
 
     nb = blocks(me)
-    loads = [("x", a, n) for a, n in nb] + [("w", 0, 256), ("w", 256, 256), ("w2", 512, 128)]
-    ltok = []
+    loads = []
+    for w in CFG["l" + role].split():
+        if w == "x":
+            loads += [("x", a, n) for a, n in xblocks(me)]
+        else:
+            loads += [("w", 0, 256), ("w", 256, 256), ("w2", 512, 128)]
+    xtok, wtok = [], {}
     for i, (k, a, n) in enumerate(loads):
-        s = "ld%d" % i
         q = dmaq[i % 2][1]
         if k == "x":
-            q.dma_start(T.xraw[:, 4 * a:4 * (a + n)], T.x[:, 4 * a:4 * (a + n)]).then_inc(T.sem[s], 16)
+            q.dma_start(T.xraw[:, 4 * a:4 * (a + n)], T.x[:, 4 * a:4 * (a + n)]).then_inc(T.sem["ld%d" % i], 16)
         elif k == "w":
-            q.dma_start(T.wraw[:, 4 * a:4 * (a + n)], T.w1[:, 4 * a:4 * (a + n)]).then_inc(T.sem[s], 16)
+            q.dma_start(T.wraw[:, 4 * a:4 * (a + n)], T.w1[:, 4 * a:4 * (a + n)]).then_inc(T.sem["ld%d" % i], 16)
         else:
-            q.dma_start(T.wraw[:, 4 * a:4 * (a + n)], T.w2[:, 0:4 * n]).then_inc(T.sem[s], 16)
-        ltok.append((s, 16))
-    xtok, wtok = None, []
+            q.dma_start(T.wraw[:, 4 * a:4 * (a + n)], T.w2[:, 0:4 * n]).then_inc(T.sem["ld%d" % i], 16)
     for i, (k, a, n) in enumerate(loads):
+        lt = [("ld%d" % i, 16)]
         if k == "x":
             oo = off[me] + a
-            xtok = ve([ltok[i]], lambda: g.vector.quantize_mx(
-                T.xq[:, oo:oo + n], T.xs[:, oo:oo + n], T.xraw[:, 4 * a:4 * (a + n)]))
+            xtok.append(ve(lt, lambda: g.vector.quantize_mx(
+                T.xq[:, oo:oo + n], T.xs[:, oo:oo + n], T.xraw[:, 4 * a:4 * (a + n)])))
         else:
-            wtok.append(ve([ltok[i]], lambda: g.vector.quantize_mx(
-                T.wq0[:, a:a + n], T.ws0[:, a:a + n], T.wraw[:, 4 * a:4 * (a + n)])))
+            t = ve(lt, lambda: g.vector.quantize_mx(
+                T.wq0[:, a:a + n], T.ws0[:, a:a + n], T.wraw[:, 4 * a:4 * (a + n)]))
+            for j in range(a // 128, (a + n) // 128):
+                wtok[j] = t
 
     nls = [0]
-    o0, o1 = off[me], off[me] + wid[me]
 
     def fused(trs):
         g.remote_dma_fused(trs, local_sem=T.sem["ls"])
 
-    wait("g", g, [xtok])
     ds, ms = xmasks(me)
-    rs = T.sem["ar_x%d" % pos]
-    for codes in (True, False):
+
+    def sendx(i, codes):
+        a, n = xblocks(me)[i]
+        o0, o1 = off[me] + a, off[me] + a + n
+        wait("g", g, [xtok[i]])
+        rs = T.sem["ar_x%d_%d" % (pos, i)]
+
         def view():
             return T.xq[:, o0:o1].bitcast(U8) if codes else T.xs[:, o0:o1]
         if ms[0] == ms[1]:
@@ -167,35 +188,57 @@ def rank_program(g, core, T, topo):
             fused([RemoteDMATransfer(dst_ids=[did(d)], dma_engine_mask=m, remote_sem=rs,
                                      srcs=[view()], dsts=[view()]) for d, m in zip(ds, ms)])
             nls[0] += count(ms[0]) + count(ms[1])
-    wait("g", g, [wtok[-1]])
-    pm = topo.mask(core, cm(peer))
-    rid, pid = topo.addr(cm(peer), core)
-    g.remote_dma(T.wq1[:].bitcast(U8), T.wq0[:].bitcast(U8), T.sem["ar_w"], T.sem["ls"], pid, rid, pm)
-    g.remote_dma(T.ws1[:], T.ws0[:], T.sem["ar_w"], T.sem["ls"], pid, rid, pm)
-    nls[0] += 2 * count(pm)
 
-    xarr = {me: xtok}
-    for r in others:
-        d2, m2 = xmasks(r)
-        xarr[r] = ("ar_x%d" % grp.index(r), 2 * count(m2[d2.index(me)]))
-    warr = ("ar_w", 2 * count(topo.mask(cm(peer), core)))
+    def sendw():
+        pm = mask(me, peer)
+        wait("g", g, sorted(wtok.values(), key=lambda t: t[1]))
+        rid, pid = topo.addr(cm(peer), core)
+        g.remote_dma(T.wq1[:].bitcast(U8), T.wq0[:].bitcast(U8), T.sem["ar_w"], T.sem["ls"], pid, rid, pm)
+        g.remote_dma(T.ws1[:], T.ws0[:], T.sem["ar_w"], T.sem["ls"], pid, rid, pm)
+        nls[0] += 2 * count(pm)
+
+    for w in CFG["s" + role].split():
+        if w[0] == "x":
+            for i in range(len(xblocks(me))):
+                for z in w[1:]:
+                    sendx(i, z == "c")
+        else:
+            sendw()
+
+    warr = ("ar_w", 2 * count(mask(peer, me)))
+
+    def xdeps(r, p, m):
+        out = []
+        for i, (a, n) in enumerate(xblocks(r)):
+            if p < a + n and a < p + m:
+                if r == me:
+                    out.append(xtok[i])
+                else:
+                    d2, m2 = xmasks(r)
+                    out.append(("ar_x%d_%d" % (grp.index(r), i), 2 * count(m2[d2.index(me)])))
+        return out
 
     own = (off[me], wid[me], [(me, 0, wid[me])])
-    big = sorted(others, key=lambda r: -wid[r])
-    oth = []
-    if sum(wid[r] for r in others) <= 256 and abs(grp.index(others[0]) - grp.index(others[1])) == 1:
-        oth.append([(off[others[0]], sum(wid[r] for r in others), [(r, 0, wid[r]) for r in others])])
-    else:
-        for r in big:
-            oth.append([(off[r] + a, n, [(r, a, n)]) for a, n in blocks(r)])
-    plan = [(0, own)]
-    for chunks in oth:
-        plan += [(0, ch) for ch in chunks]
-        plan += [(1, ch) for ch in chunks]
-    plan.append((1, own))
+    adjacent = abs(grp.index(others[0]) - grp.index(others[1])) == 1
+    if on_chip and adjacent and sum(wid[r] for r in others) <= 256:
+        role = "near0"
+    plan = []
+    for w in CFG[role].split():
+        if w[0] == "o":
+            chs = [own]
+        elif w[0] == "m":
+            chs = [(off[others[0]], sum(wid[r] for r in others), [(r, 0, wid[r]) for r in others])]
+        else:
+            rs = sorted([r for r in others if (w[0] == "s") or (r in on_chip) == (w[0] == "n")], key=lambda r: wid[r])
+            chs = [(off[r] + a, n, [(r, a, n)]) for r in rs for a, n in blocks(r)]
+        if w[1] == "B":
+            for ch in chs:
+                plan += [(0, ch), (1, ch)]
+        else:
+            plan += [("OP".index(w[1]), ch) for ch in chs]
 
     zfree = [None] * ZB
-    yfree = [None] * 2
+    yfree = [None] * (8 - ZB)
     zi, yi, ui = [0], [0], [0]
     hq = {}
 
@@ -205,7 +248,7 @@ def rank_program(g, core, T, topo):
     def unit(side, ch, between):
         a, n, parts = ch
         W, S, H, HQ, HS = [(T.wq0, T.ws0, T.h0, T.hq0, T.hs0), (T.wq1, T.ws1, T.h1, T.hq1, T.hs1)][side]
-        xdeps = [xarr[r] for r, p, m in parts]
+        xd = [d for r, p, m in parts for d in xdeps(r, p, m)]
         acts = []
         ui[0] += 1
         for b in range(4):
@@ -213,11 +256,11 @@ def rank_program(g, core, T, topo):
                 between()
             k = zi[0] % ZB
             zi[0] += 1
-            wd = warr if side else wtok[b // 2]
-            z = te([wd, zfree[k]] + xdeps, lambda: g.tensor.matmul_mx(
+            wd = warr if side else wtok[b]
+            z = te([wd, zfree[k]] + xd, lambda: g.tensor.matmul_mx(
                 bank(k, n), W[:, 128 * b:128 * b + 128], S[:, 128 * b:128 * b + 128],
                 T.xq[:, a:a + n], T.xs[:, a:a + n], True, True))
-            onv = b in ((1, 3) if ui[0] % 2 else (2,))
+            onv = b in CFG["ON"][ui[0] % len(CFG["ON"])]
             if onv:
                 t = ve([z], lambda: g.vector.tensor_scalar(
                     H[:, 4 * a + b:4 * (a + n):4], bank(k, n), 0.0, C, AluOpType.max, AluOpType.mult))
@@ -231,23 +274,21 @@ def rank_program(g, core, T, topo):
 
     def second(ch):
         a, n, parts = ch
-        k = yi[0] % 2
+        k = yi[0] % (8 - ZB)
         yi[0] += 1
-        te([wtok[-1], hq[(0, a)], yfree[k]], lambda: g.tensor.matmul_mx(
+        te([wtok[4], hq[(0, a)], yfree[k]], lambda: g.tensor.matmul_mx(
             bank(ZB + k, n), T.wq0[:, 512:640], T.ws0[:, 512:640], T.hq0[:, a:a + n], T.hs0[:, a:a + n], True, False))
         t = te([warr, hq[(1, a)]], lambda: g.tensor.matmul_mx(
             bank(ZB + k, n), T.wq1[:, 512:640], T.ws1[:, 512:640], T.hq1[:, a:a + n], T.hs1[:, a:a + n], False, True))
         return k, t
 
-    def ymask(src, dst):
-        return topo.mask(cm(src), cm(dst))
-
     def finish(ch):
         a, n, parts = ch
         k, t = second(ch)
-        if parts[0][0] == me:
-            return k, t
-        cp = sc([t], lambda: g.scalar.activation(T.yout[:, a:a + n], bank(ZB + k, n), ActivationFunctionType.Copy))
+        if CFG["cp"] == "sc":
+            cp = sc([t], lambda: g.scalar.activation(T.yout[:, a:a + n], bank(ZB + k, n), ActivationFunctionType.Copy))
+        else:
+            cp = ve([t], lambda: g.vector.tensor_copy(T.yout[:, a:a + n], bank(ZB + k, n)))
         yfree[k] = cp
         wait("g", g, [cp])
         for r, p, m in parts:
@@ -255,12 +296,10 @@ def rank_program(g, core, T, topo):
             slot = [q for q in grp if q != r].index(me)
             bi = [x[0] for x in blocks(r)].index(p)
             rid, pid = topo.addr(cm(r), core)
-            mk = ymask(me, r)
-            dst = T["yin%d" % slot]
-            g.remote_dma(dst[:, p:p + m], T.yout[:, c0:c0 + m], T.sem["ar_y%d_%d" % (slot, bi)], T.sem["ls"],
-                         pid, rid, mk)
+            mk = mask(me, r)
+            g.remote_dma(T["yin%d" % slot][:, p:p + m], T.yout[:, c0:c0 + m], T.sem["ar_y%d_%d" % (slot, bi)],
+                         T.sem["ls"], pid, rid, mk)
             nls[0] += count(mk)
-        return None
 
     pend = [None]
 
@@ -271,22 +310,21 @@ def rank_program(g, core, T, topo):
 
     for side, ch in plan:
         unit(side, ch, flush)
-        flush()
-        if side == 1:
+        if side == 1 and ch is not own:
             pend[0] = ch
-    k, t = finish(pend[0])
+    k, t = second(own)
+    flush()
 
-    near = sorted(range(2), key=lambda s: -count(topo.mask(cm(others[s]), core)))
+    near = sorted(range(2), key=lambda s: -count(mask(others[s], me)))
     fins = []
     for bi, (a, n) in enumerate(nb):
         s = near[0]
-        u = ve([t, ("ar_y%d_%d" % (s, bi), count(ymask(others[s], me)))], lambda: g.vector.tensor_tensor(
+        fins.append(ve([t, ("ar_y%d_%d" % (s, bi), count(mask(others[s], me)))], lambda: g.vector.tensor_tensor(
             T.acc[:, a:a + n], T.ps[:, 512 * (ZB + k) + a:512 * (ZB + k) + a + n], T["yin%d" % s][:, a:a + n],
-            AluOpType.add))
-        fins.append(u)
+            AluOpType.add)))
     for bi, (a, n) in enumerate(nb):
         s = near[1]
-        u = ve([fins[bi], ("ar_y%d_%d" % (s, bi), count(ymask(others[s], me)))], lambda: g.vector.tensor_tensor(
+        u = ve([fins[bi], ("ar_y%d_%d" % (s, bi), count(mask(others[s], me)))], lambda: g.vector.tensor_tensor(
             T.fin[:, a:a + n], T.acc[:, a:a + n], T["yin%d" % s][:, a:a + n], AluOpType.add))
         qn, q = dmaq[bi % 2]
         wait(qn, q, [u])

from concourse.bass import DstId, RemoteDMATransfer
from concourse.mybir import dt, AluOpType, ActivationFunctionType

U8 = dt.uint8
SCRATCH = {
    "xraw": ("sbuf", [128, 1536], "bfloat16"),
    "wraw": ("sbuf", [128, 2560], "bfloat16"),
    "xq": ("sbuf", [128, 640], "float8_e4m3fn_x4"),
    "xs": ("sbuf", [128, 640], "uint8"),
    "wq0": ("sbuf", [128, 640], "float8_e4m3fn_x4"),
    "ws0": ("sbuf", [128, 640], "uint8"),
    "wq1": ("sbuf", [128, 640], "float8_e4m3fn_x4"),
    "ws1": ("sbuf", [128, 640], "uint8"),
    "h0": ("sbuf", [128, 2560], "bfloat16"),
    "h1": ("sbuf", [128, 2560], "bfloat16"),
    "hq0": ("sbuf", [128, 640], "float8_e4m3fn_x4"),
    "hs0": ("sbuf", [128, 640], "uint8"),
    "hq1": ("sbuf", [128, 640], "float8_e4m3fn_x4"),
    "hs1": ("sbuf", [128, 640], "uint8"),
    "yout": ("sbuf", [128, 640], "float32"),
    "yin0": ("sbuf", [128, 384], "float32"),
    "yin1": ("sbuf", [128, 384], "float32"),
    "acc": ("sbuf", [128, 384], "float32"),
    "fin": ("sbuf", [128, 384], "float32"),
    "ps": ("psum", [128, 4096], "float32"),
}
CFG = dict(ZB=6, LATE=3, CUT=270, XCUT=270, far="oO sB oP", near="oO nO fO nP fP oP", near0="oO mB oP",
           sfar="xc w xs", snear="xcs w", lfar="x w", lnear="x w", ON=((1, 3),), cp="sc")
C = 0.029
SEMAPHORES = (["ld%d" % i for i in range(5)] + ["st%d" % i for i in range(2)]
              + ["ar_x%d_%d" % (s, b) for s in range(3) for b in range(2)]
              + ["ar_w", "ls", "te", "ve", "sc"]
              + ["ar_y%d_%d" % (s, b) for s in range(2) for b in range(2)])


def grid(T, topo):
    wid, cores, n = T.tables["WID"], T.cores, len(T.cores)
    half = sum(wid) // 2

    def home(r):
        return (topo.host(cores[r]), topo.chip(cores[r]))
    for bits in range(1, 1 << n, 2):
        a = [r for r in range(n) if bits >> r & 1]
        b = [r for r in range(n) if not bits >> r & 1]
        if len(a) != len(b) or sum(wid[r] for r in a) != half:
            continue
        left, pairs = list(b), []
        for r in a:
            for q in left:
                if home(q) == home(r):
                    pairs.append(q)
                    left.remove(q)
                    break
        if len(pairs) == len(a):
            return a, pairs
    raise ValueError("no grid")


def count(m):
    return bin(m).count("1")


def cut(n, limit):
    return [(0, n // 2), (n // 2, n // 2)] if n > limit else [(0, n)]


def rank_program(g, core, T, topo):
    me = T.rank_of(core)
    if me is None:
        return
    ZB, LATE = CFG["ZB"], CFG["LATE"]
    wid = T.tables["WID"]
    ga, gb = grid(T, topo)
    grp = ga if me in ga else gb
    pos = grp.index(me)
    peer = (gb if me in ga else ga)[pos]
    others = [r for r in grp if r != me]
    off = {}
    o = 0
    for r in grp:
        off[r] = o
        o += wid[r]

    def blocks(r):
        return cut(wid[r], CFG["CUT"])

    def xblocks(r):
        return cut(wid[r], CFG["XCUT"])

    def cm(r):
        return T.cores[r]

    def mask(a, b):
        return topo.mask(cm(a), cm(b))

    def xmasks(src):
        ds = [r for r in grp if r != src]
        ms = [mask(src, d) for d in ds]
        if ms[0] != ms[1]:
            i = 0 if count(ms[0]) > count(ms[1]) else 1
            ms[i] &= ~ms[1 - i]
        return ds, ms

    def did(r):
        rid, pid = topo.addr(cm(r), core)
        return DstId(rid=rid, pnc=pid)

    on_chip = [r for r in others if mask(r, me) == mask(peer, me)]
    role = "near" if on_chip else "far"

    known, done = {}, {"te": 0, "ve": 0, "sc": 0}
    final = []

    def wait(qn, q, deps):
        for tok in deps:
            if tok is None:
                continue
            s, v = tok
            if known.get((qn, s), 0) < v:
                q.wait_ge(T.sem[s], v)
                known[(qn, s)] = v

    def run(qn, q, deps, fn):
        wait(qn, q, deps)
        fn().then_inc(T.sem[qn], 1)
        done[qn] += 1
        return (qn, done[qn])

    def te(deps, fn):
        return run("te", g.tensor, deps, fn)

    def ve(deps, fn):
        return run("ve", g.vector, deps, fn)

    def sc(deps, fn):
        return run("sc", g.scalar, deps, fn)

    dmaq = [("sync", g.sync), ("sc", g.scalar)]

    nb = blocks(me)
    loads = []
    for w in CFG["l" + role].split():
        if w == "x":
            loads += [("x", a, n) for a, n in xblocks(me)]
        else:
            loads += [("w", 0, 256), ("w", 256, 256), ("w2", 512, 128)]
    xtok, wtok = [], {}
    for i, (k, a, n) in enumerate(loads):
        q = dmaq[i % 2][1]
        if k == "x":
            q.dma_start(T.xraw[:, 4 * a:4 * (a + n)], T.x[:, 4 * a:4 * (a + n)]).then_inc(T.sem["ld%d" % i], 16)
        elif k == "w":
            q.dma_start(T.wraw[:, 4 * a:4 * (a + n)], T.w1[:, 4 * a:4 * (a + n)]).then_inc(T.sem["ld%d" % i], 16)
        else:
            q.dma_start(T.wraw[:, 4 * a:4 * (a + n)], T.w2[:, 0:4 * n]).then_inc(T.sem["ld%d" % i], 16)
    for i, (k, a, n) in enumerate(loads):
        lt = [("ld%d" % i, 16)]
        if k == "x":
            oo = off[me] + a
            xtok.append(ve(lt, lambda: g.vector.quantize_mx(
                T.xq[:, oo:oo + n], T.xs[:, oo:oo + n], T.xraw[:, 4 * a:4 * (a + n)])))
        else:
            t = ve(lt, lambda: g.vector.quantize_mx(
                T.wq0[:, a:a + n], T.ws0[:, a:a + n], T.wraw[:, 4 * a:4 * (a + n)]))
            for j in range(a // 128, (a + n) // 128):
                wtok[j] = t

    nls = [0]

    def fused(trs):
        g.remote_dma_fused(trs, local_sem=T.sem["ls"])

    ds, ms = xmasks(me)

    def sendx(i, codes):
        a, n = xblocks(me)[i]
        o0, o1 = off[me] + a, off[me] + a + n
        wait("g", g, [xtok[i]])
        rs = T.sem["ar_x%d_%d" % (pos, i)]

        def view():
            return T.xq[:, o0:o1].bitcast(U8) if codes else T.xs[:, o0:o1]
        if ms[0] == ms[1]:
            fused([RemoteDMATransfer(dst_ids=[did(d) for d in ds], dma_engine_mask=ms[0], remote_sem=rs,
                                     srcs=[view()], dsts=[view() for d in ds])])
            nls[0] += count(ms[0])
        else:
            fused([RemoteDMATransfer(dst_ids=[did(d)], dma_engine_mask=m, remote_sem=rs,
                                     srcs=[view()], dsts=[view()]) for d, m in zip(ds, ms)])
            nls[0] += count(ms[0]) + count(ms[1])

    def sendw():
        pm = mask(me, peer)
        wait("g", g, sorted(wtok.values(), key=lambda t: t[1]))
        rid, pid = topo.addr(cm(peer), core)
        g.remote_dma(T.wq1[:].bitcast(U8), T.wq0[:].bitcast(U8), T.sem["ar_w"], T.sem["ls"], pid, rid, pm)
        g.remote_dma(T.ws1[:], T.ws0[:], T.sem["ar_w"], T.sem["ls"], pid, rid, pm)
        nls[0] += 2 * count(pm)

    for w in CFG["s" + role].split():
        if w[0] == "x":
            for i in range(len(xblocks(me))):
                for z in w[1:]:
                    sendx(i, z == "c")
        else:
            sendw()

    warr = ("ar_w", 2 * count(mask(peer, me)))

    def xdeps(r, p, m):
        out = []
        for i, (a, n) in enumerate(xblocks(r)):
            if p < a + n and a < p + m:
                if r == me:
                    out.append(xtok[i])
                else:
                    d2, m2 = xmasks(r)
                    out.append(("ar_x%d_%d" % (grp.index(r), i), 2 * count(m2[d2.index(me)])))
        return out

    own = (off[me], wid[me], [(me, 0, wid[me])])
    adjacent = abs(grp.index(others[0]) - grp.index(others[1])) == 1
    if on_chip and adjacent and sum(wid[r] for r in others) <= 256:
        role = "near0"
    plan = []
    for w in CFG[role].split():
        if w[0] == "o":
            chs = [own]
        elif w[0] == "m":
            chs = [(off[others[0]], sum(wid[r] for r in others), [(r, 0, wid[r]) for r in others])]
        else:
            rs = sorted([r for r in others if (w[0] == "s") or (r in on_chip) == (w[0] == "n")], key=lambda r: wid[r])
            chs = [(off[r] + a, n, [(r, a, n)]) for r in rs for a, n in blocks(r)]
        if w[1] == "B":
            for ch in chs:
                plan += [(0, ch), (1, ch)]
        else:
            plan += [("OP".index(w[1]), ch) for ch in chs]

    zfree = [None] * ZB
    yfree = [None] * (8 - ZB)
    zi, yi, ui = [0], [0], [0]
    hq = {}

    def bank(b, n):
        return T.ps[:, 512 * b:512 * b + n]

    def unit(side, ch, between):
        a, n, parts = ch
        W, S, H, HQ, HS = [(T.wq0, T.ws0, T.h0, T.hq0, T.hs0), (T.wq1, T.ws1, T.h1, T.hq1, T.hs1)][side]
        xd = [d for r, p, m in parts for d in xdeps(r, p, m)]
        acts = []
        ui[0] += 1
        for b in range(4):
            if b == LATE:
                between()
            k = zi[0] % ZB
            zi[0] += 1
            wd = warr if side else wtok[b]
            z = te([wd, zfree[k]] + xd, lambda: g.tensor.matmul_mx(
                bank(k, n), W[:, 128 * b:128 * b + 128], S[:, 128 * b:128 * b + 128],
                T.xq[:, a:a + n], T.xs[:, a:a + n], True, True))
            onv = b in CFG["ON"][ui[0] % len(CFG["ON"])]
            if onv:
                t = ve([z], lambda: g.vector.tensor_scalar(
                    H[:, 4 * a + b:4 * (a + n):4], bank(k, n), 0.0, C, AluOpType.max, AluOpType.mult))
            else:
                t = sc([z], lambda: g.scalar.activation(
                    H[:, 4 * a + b:4 * (a + n):4], bank(k, n), ActivationFunctionType.Relu, scale=C))
            zfree[k] = t
            acts.append(t)
        hq[(side, a)] = ve(acts, lambda: g.vector.quantize_mx(
            HQ[:, a:a + n], HS[:, a:a + n], H[:, 4 * a:4 * (a + n)]))

    def second(ch):
        a, n, parts = ch
        k = yi[0] % (8 - ZB)
        yi[0] += 1
        te([wtok[4], hq[(0, a)], yfree[k]], lambda: g.tensor.matmul_mx(
            bank(ZB + k, n), T.wq0[:, 512:640], T.ws0[:, 512:640], T.hq0[:, a:a + n], T.hs0[:, a:a + n], True, False))
        t = te([warr, hq[(1, a)]], lambda: g.tensor.matmul_mx(
            bank(ZB + k, n), T.wq1[:, 512:640], T.ws1[:, 512:640], T.hq1[:, a:a + n], T.hs1[:, a:a + n], False, True))
        return k, t

    def finish(ch):
        a, n, parts = ch
        k, t = second(ch)
        if CFG["cp"] == "sc":
            cp = sc([t], lambda: g.scalar.activation(T.yout[:, a:a + n], bank(ZB + k, n), ActivationFunctionType.Copy))
        else:
            cp = ve([t], lambda: g.vector.tensor_copy(T.yout[:, a:a + n], bank(ZB + k, n)))
        yfree[k] = cp
        wait("g", g, [cp])
        for r, p, m in parts:
            c0 = off[r] + p
            slot = [q for q in grp if q != r].index(me)
            bi = [x[0] for x in blocks(r)].index(p)
            rid, pid = topo.addr(cm(r), core)
            mk = mask(me, r)
            g.remote_dma(T["yin%d" % slot][:, p:p + m], T.yout[:, c0:c0 + m], T.sem["ar_y%d_%d" % (slot, bi)],
                         T.sem["ls"], pid, rid, mk)
            nls[0] += count(mk)

    pend = [None]

    def flush():
        if pend[0] is not None:
            finish(pend[0])
            pend[0] = None

    for side, ch in plan:
        unit(side, ch, flush)
        if side == 1 and ch is not own:
            pend[0] = ch
    k, t = second(own)
    flush()

    near = sorted(range(2), key=lambda s: -count(mask(others[s], me)))
    fins = []
    for bi, (a, n) in enumerate(nb):
        s = near[0]
        fins.append(ve([t, ("ar_y%d_%d" % (s, bi), count(mask(others[s], me)))], lambda: g.vector.tensor_tensor(
            T.acc[:, a:a + n], T.ps[:, 512 * (ZB + k) + a:512 * (ZB + k) + a + n], T["yin%d" % s][:, a:a + n],
            AluOpType.add)))
    for bi, (a, n) in enumerate(nb):
        s = near[1]
        u = ve([fins[bi], ("ar_y%d_%d" % (s, bi), count(mask(others[s], me)))], lambda: g.vector.tensor_tensor(
            T.fin[:, a:a + n], T.acc[:, a:a + n], T["yin%d" % s][:, a:a + n], AluOpType.add))
        qn, q = dmaq[bi % 2]
        wait(qn, q, [u])
        q.dma_start(T.y[:, a:a + n], T.fin[:, a:a + n]).then_inc(T.sem["st%d" % bi], 16)
        final.append(("st%d" % bi, 16))
    final += [("ls", nls[0]), ("te", done["te"]), ("ve", done["ve"]), ("sc", done["sc"])]
    wait("g", g, final)
